import numpy as np
import ml_dtypes


def mxq(x, axis, fmt="e4m3"):
    dtype, down = {"e4m3": (ml_dtypes.float8_e4m3fn, 7), "e5m2": (ml_dtypes.float8_e5m2, 14)}[fmt]
    v = np.moveaxis(np.asarray(x, np.float32).astype(ml_dtypes.bfloat16).astype(np.float64), axis, -1)
    blocks = v.reshape(v.shape[:-1] + (-1, 32))
    amax = np.abs(blocks).max(-1, keepdims=True)
    byte = np.maximum(np.where(amax > 0, np.frexp(amax)[1] - 1 + 127, 0) - down, 1)
    scale = np.exp2(byte - 127.0)
    codes = (blocks / scale).astype(np.float32).astype(dtype).astype(np.float64)
    return np.moveaxis((codes * scale).reshape(v.shape), -1, axis)


WIDE = False


def mx_kscale(k):
    if not WIDE:
        return np.ones(k)
    levels = np.array([10, -10, 5, -5, 0])
    if k % 512:
        return np.exp2(np.random.permutation(np.resize(levels, k // 32))).repeat(32)
    a = np.empty((k // 512, 16))
    for p in range(k // 512):
        a[p, :8] = np.random.permutation(np.resize(levels, 8))
        for g in range(8):
            far = levels[np.abs(levels - a[p, g]) >= 10]
            a[p, g + 8] = far[np.random.randint(len(far))]
    return np.exp2(a.ravel()).repeat(32)


def f64(x):
    return np.asarray(x).astype(np.float64)


def striped(idx):
    return np.tile(idx.reshape(-1, 16).T, (8, 1)).astype(np.uint16)


def unstriped(offs):
    return offs[:16].T.reshape(-1).astype(np.int64)


def pack_weight(w):
    k, n = w.shape
    w = f64(np.asarray(w, np.float32).astype(ml_dtypes.bfloat16)).reshape(k // 32, 32, n)
    amax = np.abs(w).max(1)
    byte = np.clip(np.where(amax > 0, np.frexp(amax)[1] - 1 + 127 - 7, 1), 1, 254)
    scaled = (w * np.exp2(127.0 - byte)[:, None, :]).reshape(k, n).astype(np.float32)
    words = np.ascontiguousarray(scaled.reshape(k // 512, 128, 4, n).transpose(0, 1, 3, 2)).astype(ml_dtypes.float8_e4m3fn).view(np.uint8)
    return words, np.ascontiguousarray(byte.astype(np.uint8).reshape(k // 512, 16, n))


def unpack_weight(words, scales):
    g, p, n, _ = words.shape
    vals = np.ascontiguousarray(words).view(ml_dtypes.float8_e4m3fn).astype(np.float64) * np.repeat(np.exp2(scales.astype(np.float64) - 127.0), 8, axis=1)[..., None]
    return vals.transpose(0, 1, 3, 2).reshape(g * 512, n)


K, T, S, N, H, U = 1024, 2048, 512, 128, 512, 1024


def setup_inputs():
    n = np.random.standard_normal
    s = mx_kscale(K)[:, None]
    u = mx_kscale(H)
    packed_xT = pack_weight(n((K, T)) * s)
    return {
        "x_words": packed_xT[0],
        "x_scales": packed_xT[1],
        "w1": (n((K, H)) / np.sqrt(K) / s).astype(np.float32),
        "w2": (n((K, H)) / np.sqrt(K) / s).astype(np.float32),
        "old": (0.7 * n((H, U))).astype(np.float32),
        "unit": (np.random.uniform(0.6, 1.4, (H, 1)) * u[:, None]).astype(np.float32),
        "w3": (n((H, N)) / np.sqrt(H) / u[:, None]).astype(np.float32),
        "offs": striped(np.random.permutation(T)[:S]),
        "snd": striped(np.random.permutation(np.concatenate([np.arange(S), np.random.randint(0, S, U - S)]))),
        "oth": striped(np.random.permutation(np.concatenate([np.arange(S), np.random.randint(0, S, U - S)]))),
    }


def reference(x_words, x_scales, w1, w2, old, unit, w3, offs, snd, oth):
    xq = unpack_weight(x_words, x_scales)[:, unstriped(offs)]
    y = mxq(f64(w1), 0, "e4m3").T @ xq
    ys = y[:, unstriped(snd)]
    yo = y[:, unstriped(oth)]
    dlt = ys - yo
    z1 = mxq(f64(w2), 0, "e4m3").T @ xq
    zo = z1[:, unstriped(oth)]
    wex = dlt * zo
    hid = f64(unit) * (wex + f64(old))
    return mxq(f64(w3), 0, "e4m3").T @ mxq(hid, 0, "e4m3")

@@ -1,0 +1,252 @@
+from contextlib import ExitStack
+
+import concourse.mybir as mybir
+from concourse.masks import make_identity
+
+K, T, S, N, H, U = 1024, 2048, 512, 128, 512, 1024
+FLOPS = 2 * (2 * K * H * S) + 2 * H * N * U
+
+F32 = mybir.dt.float32
+BF16 = mybir.dt.bfloat16
+I32 = mybir.dt.int32
+U32 = mybir.dt.uint32
+U16 = mybir.dt.uint16
+U8 = mybir.dt.uint8
+FP8X4 = mybir.dt.float8_e4m3fn_x4
+MULT = mybir.AluOpType.mult
+COPY = mybir.ActivationFunctionType.Copy
+
+P = 128
+PACK = 4
+PASSES = K // (P * PACK)
+BLOCKS = H // P
+SPARE = 32
+QUARTER = 256
+
+
+def tile_picked_ydiffex_gate_p_kernel(
+    tc, x_words, x_scales, w1, w2, old, unit, w3, offs, snd, oth, out
+):
+    nc = tc.nc
+    with ExitStack() as ctx:
+        keep = ctx.enter_context(tc.tile_pool(name="keep", bufs=1))
+        ring = ctx.enter_context(tc.tile_pool(name="ring", bufs=3))
+        psum = ctx.enter_context(tc.psum_pool(name="psum", bufs=1))
+        psum_sum = ctx.enter_context(tc.psum_pool(name="psum_sum", bufs=4))
+        psum_back = ctx.enter_context(tc.psum_pool(name="psum_back", bufs=2))
+
+        offs_sb = keep.tile([P, S // 16], U16, name="offs_sb")
+        snd_sb = keep.tile([P, U // 16], U16, name="snd_sb")
+        oth_sb = keep.tile([P, U // 16], U16, name="oth_sb")
+        nc.sync.dma_start(offs_sb[:], offs)
+
+        unit_sb = keep.tile([P, PACK], F32, name="unit_sb")
+        nc.gpsimd.dma_start(unit_sb[:], unit.rearrange("(p t) o -> p (t o)", t=PACK))
+
+        table_scales = keep.tile([P, T], U8, name="table_scales", align_bytes=64)
+        nc.vector.memset(table_scales[:].bitcast(I32), 0)
+        for quad in range(4):
+            nc.scalar.dma_start(
+                table_scales[32 * quad : 32 * quad + 4 * PASSES, :].bitcast(I32),
+                x_scales[:, 4 * quad : 4 * quad + 4, :].bitcast(I32),
+            )
+        table_words = []
+        for g in range(PASSES):
+            words = keep.tile([P, T], I32, name="table_words%d" % g, align_bytes=64)
+            nc.sync.dma_start(words[:], x_words[g].rearrange("p n t -> p (n t)").bitcast(I32))
+            table_words.append(words)
+
+        def load_weight_block(w, label, b):
+            raw = keep.tile([P, PASSES, PACK, P], F32, name="raw_%s%d" % (label, b))
+            for g in range(PASSES):
+                rows = w[g * P * PACK : (g + 1) * P * PACK, b * P : (b + 1) * P]
+                nc.sync.dma_start(raw[:, g], rows.rearrange("(p j) c -> p j c", j=PACK))
+            return raw
+
+        def load_old(b):
+            kept = keep.tile([P, U], F32, name="old%d" % b)
+            nc.sync.dma_start(kept[:], old[b * P : (b + 1) * P, :])
+            return kept
+
+        raw_w2 = [load_weight_block(w2, "w2", 0)]
+        raw_w1 = [load_weight_block(w1, "w1", 0)]
+        nc.sync.dma_start(oth_sb[:], oth)
+        nc.sync.dma_start(snd_sb[:], snd)
+        old_sb = []
+        for b in range(1, BLOCKS):
+            raw_w2.append(load_weight_block(w2, "w2", b))
+            raw_w1.append(load_weight_block(w1, "w1", b))
+            old_sb.append(load_old(b - 1))
+        old_sb.append(load_old(BLOCKS - 1))
+        raw_w3 = keep.tile([P, 1, PACK, N], F32, name="raw_w3")
+        nc.sync.dma_start(raw_w3[:, 0], w3.rearrange("(p j) c -> p j c", j=PACK))
+
+        ident = keep.tile([P, P], F32, name="ident")
+        make_identity(nc, ident[:])
+
+        windows = {}
+        for b in range(BLOCKS):
+            for label in ("z", "y", "q"):
+                window = keep.tile([P, S + SPARE], F32, name="window_%s%d" % (label, b))
+                nc.gpsimd.memset(window[:, S:], 0.0)
+                windows[label, b] = window
+
+        picked_words = []
+        picked_scales = keep.tile([P, S], U8, name="picked_scales", align_bytes=64)
+        for g in range(PASSES):
+            picked = keep.tile([P, S], U32, name="picked_words%d" % g, align_bytes=64)
+            nc.vector.tensor_copy(picked[:], table_words[g][:].bitcast(U32).indirect(offs_sb[:]))
+            picked_words.append(picked)
+            if g == 0:
+                nc.vector.tensor_copy(picked_scales[:], table_scales[:].indirect(offs_sb[:]))
+
+        def round_and_group(raw, label, on_scalar):
+            passes = raw.shape[1]
+            grouped = keep.tile([P, passes * P * PACK], BF16, name="grouped_" + label, tag="stage_" + label, align_bytes=64)
+            dst = grouped[:].rearrange("p (g c i t) -> p g c t i", g=passes, i=4, t=PACK)
+            src = raw.rearrange("p g t (c i) -> p g c t i", i=4)
+            if on_scalar:
+                nc.scalar.activation(dst[:, 0], src[:, 0], COPY)
+            else:
+                nc.vector.tensor_copy(dst, src)
+            return grouped
+
+        def quantize(grouped, label):
+            width = grouped.shape[1] // PACK
+            codes = keep.tile([P, width], U32, name="codes_" + label, align_bytes=64)
+            scales = keep.tile([P, width], U8, name="scales_" + label, align_bytes=64)
+            nc.vector.quantize_mx(out=codes[:].bitcast(FP8X4), scales=scales[:], in_=grouped[:])
+            return codes, scales
+
+        def first_product(raw, label, b):
+            name = "%s%d" % (label, b)
+            if b == 0:
+                grouped = [round_and_group(raw[:, g : g + 1], "%s_%d" % (name, g), label == "z") for g in range(PASSES)]
+                quantized = [quantize(grouped[g], "%s_%d" % (name, g)) for g in range(PASSES)]
+                operands = [(codes[:], scales[:]) for codes, scales in quantized]
+            else:
+                codes, scales = quantize(round_and_group(raw[:], name, False), name)
+                operands = [(codes[:, g * P : (g + 1) * P], scales[:, g * P : (g + 1) * P]) for g in range(PASSES)]
+            acc = psum.tile([P, S], F32, name="acc_" + name, tag="acc_" + label)
+            for g in range(PASSES):
+                nc.tensor.matmul_mx(
+                    out=acc[:],
+                    lhsT=operands[g][0].bitcast(FP8X4),
+                    lhsT_scale=operands[g][1],
+                    rhs=picked_words[g][:].bitcast(FP8X4),
+                    rhs_scale=picked_scales[4 * g : P, :],
+                    start=(g == 0),
+                    stop=(g == PASSES - 1),
+                )
+            return acc
+
+        def make_windows(b):
+            acc_z = first_product(raw_w2[b], "z", b)
+            nc.scalar.activation(windows["z", b][:, :S], acc_z[:], COPY)
+            acc_y = first_product(raw_w1[b], "y", b)
+            if b == 0:
+                nc.vector.tensor_copy(windows["y", b][:, :S], acc_y[:])
+                nc.vector.scalar_tensor_tensor(
+                    windows["q", b][:, :S], acc_y[:], -1.0, windows["z", b][:, :S], MULT, MULT
+                )
+            else:
+                nc.scalar.activation(windows["y", b][:, :S], acc_y[:], COPY)
+                nc.vector.scalar_tensor_tensor(
+                    windows["q", b][:, :S], acc_z[:], -1.0, windows["y", b][:, :S], MULT, MULT
+                )
+
+        unit_ps = psum_back.tile([P, PACK, P], F32, name="unit_ps", tag="back")
+        for t in range(PACK):
+            nc.tensor.matmul(
+                unit_ps[:, t, :], unit_sb[:, t : t + 1].to_broadcast([P, P]), ident[:],
+                start=True, stop=True, is_transpose=True,
+            )
+        unit_row = keep.tile([P, H], F32, name="unit_row")
+        nc.scalar.activation(
+            unit_row[:].rearrange("p (n t) -> p n t", t=PACK), unit_ps[:].rearrange("p t n -> p n t"), COPY
+        )
+
+        pieces = [(0, 512), (512, 256), (768, 256)]
+        hid_t = {r0: keep.tile([P, n // P, H], BF16, name="hid_t%d" % r0) for r0, n in pieces}
+
+        def fetch(label, b, r0, n):
+            fetched = ring.tile([P, n], F32, name="fetched_" + label, tag="fetched_" + label)
+            cols = slice(r0 // 16, (r0 + n) // 16)
+            nc.scalar.activation(fetched[:], windows[label, b][:].indirect(oth_sb[:, cols]), COPY)
+            return fetched
+
+        def send(b, r0, n, gate, stage):
+            sender = keep.tile([P, n], F32, name="sender", tag="stage_" + stage, align_bytes=64)
+            cols = slice(r0 // 16, (r0 + n) // 16)
+            nc.vector.tensor_tensor(sender[:], windows["y", b][:].indirect(snd_sb[:, cols]), gate[:], MULT)
+            return sender
+
+        def add_up(b, r0, n, sender, other):
+            total = psum_sum.tile([P, n // P, P], F32, name="total", tag="total")
+            for c in range(n // P):
+                terms = (
+                    sender[:, c * P : (c + 1) * P],
+                    other[:, c * P : (c + 1) * P],
+                    old_sb[b][:, r0 + c * P : r0 + (c + 1) * P],
+                )
+                for k, term in enumerate(terms):
+                    nc.tensor.matmul(
+                        total[:, c, :], term, ident[:], start=(k == 0), stop=(k == len(terms) - 1), is_transpose=True
+                    )
+            return total
+
+        def scale_and_round(b, r0, n, total):
+            for p0, pn in pieces:
+                if r0 <= p0 < r0 + n:
+                    c0 = (p0 - r0) // P
+                    factor = unit_row[:, b * P : (b + 1) * P].unsqueeze(1).to_broadcast([P, pn // P, P])
+                    nc.vector.tensor_tensor(
+                        hid_t[p0][:, :, b * P : (b + 1) * P], total[:, c0 : c0 + pn // P, :], factor, MULT
+                    )
+
+        def last_product(r0, w3_codes, w3_scales, bank, copy):
+            p0 = max(start for start, n in pieces if start <= r0)
+            back = psum_back.tile([P, 2, 2, P], F32, name="back", tag="back")
+            for a in range(2):
+                words = hid_t[p0][:, (r0 - p0) // P + a, :].bitcast(F32)
+                for u in range(2):
+                    nc.tensor.transpose(back[:, a, u, :], words[:, u : H // 2 : 2], ident[:])
+            grouped = keep.tile([P, QUARTER * PACK], BF16, name="grouped_hid%d" % r0, align_bytes=64)
+            copy(
+                grouped[:].bitcast(F32).rearrange("p (a r u) -> p a r u", a=2, u=2),
+                back[:].rearrange("p a u r -> p a r u"),
+            )
+            codes, scales = quantize(grouped, "hid%d" % r0)
+            acc = psum.tile([P, QUARTER], F32, name="acc_out", tag=bank)
+            nc.tensor.matmul_mx(
+                out=acc[:],
+                lhsT=w3_codes[:].bitcast(FP8X4),
+                lhsT_scale=w3_scales[:],
+                rhs=codes[:].bitcast(FP8X4),
+                rhs_scale=scales[:],
+                start=True,
+                stop=True,
+            )
+            result = keep.tile([P, QUARTER], F32, name="result%d" % r0)
+            copy(result[:], acc[:])
+            nc.sync.dma_start(out[:, r0 : r0 + QUARTER], result[:])
+
+        make_windows(0)
+        for b in range(BLOCKS - 1):
+            gates = [fetch("z", b, r0, 512) for r0 in (0, 512)]
+            others = [fetch("q", b, r0, 512) for r0 in (0, 512)]
+            make_windows(b + 1)
+            for h, label in enumerate(("z", "y")):
+                sender = send(b, 512 * h, 512, gates[h], "%s%d" % (label, b + 1))
+                scale_and_round(b, 512 * h, 512, add_up(b, 512 * h, 512, sender, others[h]))
+        w3_codes, w3_scales = quantize(round_and_group(raw_w3[:], "w3", False), "w3")
+        last = BLOCKS - 1
+        for r0, n in pieces:
+            gate = fetch("z", last, r0, n)
+            other = fetch("q", last, r0, n)
+            sender = send(last, r0, n, gate, "last%d" % r0)
+            scale_and_round(last, r0, n, add_up(last, r0, n, sender, other))
+        last_product(0, w3_codes, w3_scales, "acc_z", nc.vector.tensor_copy)
+        last_product(256, w3_codes, w3_scales, "acc_y", nc.vector.tensor_copy)
+        last_product(512, w3_codes, w3_scales, "acc_z", nc.scalar.copy)
+        last_product(768, w3_codes, w3_scales, "acc_y", nc.scalar.copy)

@@ -1,7 +1,6 @@
 from contextlib import ExitStack
 
 import concourse.mybir as mybir
-from concourse.masks import make_identity
 
 K, T, S, N, H, U = 1024, 2048, 512, 128, 512, 1024
 FLOPS = 2 * (2 * K * H * S) + 2 * H * N * U
@@ -14,14 +13,15 @@ U16 = mybir.dt.uint16
 U8 = mybir.dt.uint8
 FP8X4 = mybir.dt.float8_e4m3fn_x4
 MULT = mybir.AluOpType.mult
+ADD = mybir.AluOpType.add
 COPY = mybir.ActivationFunctionType.Copy
 
 P = 128
 PACK = 4
 PASSES = K // (P * PACK)
-BLOCKS = H // P
 SPARE = 32
-QUARTER = 256
+HALF = U // 2
+FUSED_PLANES = 2
 
 
 def tile_picked_ydiffex_gate_p_kernel(
@@ -32,84 +32,65 @@ def tile_picked_ydiffex_gate_p_kernel(
         keep = ctx.enter_context(tc.tile_pool(name="keep", bufs=1))
         ring = ctx.enter_context(tc.tile_pool(name="ring", bufs=3))
         psum = ctx.enter_context(tc.psum_pool(name="psum", bufs=1))
-        psum_sum = ctx.enter_context(tc.psum_pool(name="psum_sum", bufs=4))
-        psum_back = ctx.enter_context(tc.psum_pool(name="psum_back", bufs=2))
 
         offs_sb = keep.tile([P, S // 16], U16, name="offs_sb")
         snd_sb = keep.tile([P, U // 16], U16, name="snd_sb")
         oth_sb = keep.tile([P, U // 16], U16, name="oth_sb")
         nc.sync.dma_start(offs_sb[:], offs)
 
-        unit_sb = keep.tile([P, PACK], F32, name="unit_sb")
-        nc.gpsimd.dma_start(unit_sb[:], unit.rearrange("(p t) o -> p (t o)", t=PACK))
-
         table_scales = keep.tile([P, T], U8, name="table_scales", align_bytes=64)
-        nc.vector.memset(table_scales[:].bitcast(I32), 0)
-        for quad in range(4):
-            nc.scalar.dma_start(
-                table_scales[32 * quad : 32 * quad + 4 * PASSES, :].bitcast(I32),
-                x_scales[:, 4 * quad : 4 * quad + 4, :].bitcast(I32),
-            )
-        table_words = []
-        for g in range(PASSES):
+        nc.gpsimd.memset(table_scales[:].bitcast(I32), 0)
+
+        def load_words(g):
             words = keep.tile([P, T], I32, name="table_words%d" % g, align_bytes=64)
             nc.sync.dma_start(words[:], x_words[g].rearrange("p n t -> p (n t)").bitcast(I32))
-            table_words.append(words)
+            return words
 
-        def load_weight_block(w, label, b):
-            raw = keep.tile([P, PASSES, PACK, P], F32, name="raw_%s%d" % (label, b))
-            for g in range(PASSES):
-                rows = w[g * P * PACK : (g + 1) * P * PACK, b * P : (b + 1) * P]
-                nc.sync.dma_start(raw[:, g], rows.rearrange("(p j) c -> p j c", j=PACK))
+        def load_rows(w, g, label):
+            raw = keep.tile([P, PACK, w.shape[1]], F32, name="raw_" + label, tag="raw_" + label, align_bytes=64)
+            rows = w[g * P * PACK : (g + 1) * P * PACK, :]
+            nc.sync.dma_start(raw[:], rows.rearrange("(p j) c -> p j c", j=PACK))
             return raw
 
-        def load_old(b):
-            kept = keep.tile([P, U], F32, name="old%d" % b)
-            nc.sync.dma_start(kept[:], old[b * P : (b + 1) * P, :])
-            return kept
-
-        raw_w2 = [load_weight_block(w2, "w2", 0)]
-        raw_w1 = [load_weight_block(w1, "w1", 0)]
+        raw_w1, table_words = [], []
+        for g in range(PASSES):
+            raw_w1.append(load_rows(w1, g, "w1_%d" % g))
+            if g == 0:
+                for quad in range(4):
+                    nc.sync.dma_start(
+                        table_scales[32 * quad : 32 * quad + 4 * PASSES, :].bitcast(I32),
+                        x_scales[:, 4 * quad : 4 * quad + 4, :].bitcast(I32),
+                    )
+            table_words.append(load_words(g))
         nc.sync.dma_start(oth_sb[:], oth)
         nc.sync.dma_start(snd_sb[:], snd)
+        raw_w2 = [load_rows(w2, g, "w2_%d" % g) for g in range(PASSES)]
+        unit_sb = keep.tile([P, PACK], F32, name="unit_sb")
+        nc.sync.dma_start(unit_sb[:], unit.rearrange("(p t) o -> p (t o)", t=PACK))
         old_sb = []
-        for b in range(1, BLOCKS):
-            raw_w2.append(load_weight_block(w2, "w2", b))
-            raw_w1.append(load_weight_block(w1, "w1", b))
-            old_sb.append(load_old(b - 1))
-        old_sb.append(load_old(BLOCKS - 1))
-        raw_w3 = keep.tile([P, 1, PACK, N], F32, name="raw_w3")
-        nc.sync.dma_start(raw_w3[:, 0], w3.rearrange("(p j) c -> p j c", j=PACK))
-
-        ident = keep.tile([P, P], F32, name="ident")
-        make_identity(nc, ident[:])
+        for h in range(2):
+            kept = keep.tile([P, PACK, HALF], F32, name="old%d" % h)
+            nc.sync.dma_start(kept[:], old[:, h * HALF : (h + 1) * HALF].rearrange("(p t) r -> p t r", t=PACK))
+            old_sb.append(kept)
+        raw_w3 = load_rows(w3, 0, "w3")
 
         windows = {}
-        for b in range(BLOCKS):
-            for label in ("z", "y", "q"):
-                window = keep.tile([P, S + SPARE], F32, name="window_%s%d" % (label, b))
+        for label in ("y", "z"):
+            for t in range(PACK):
+                window = keep.tile([P, S + SPARE], F32, name="window_%s%d" % (label, t))
                 nc.gpsimd.memset(window[:, S:], 0.0)
-                windows[label, b] = window
+                windows[label, t] = window
 
-        picked_words = []
-        picked_scales = keep.tile([P, S], U8, name="picked_scales", align_bytes=64)
-        for g in range(PASSES):
-            picked = keep.tile([P, S], U32, name="picked_words%d" % g, align_bytes=64)
-            nc.vector.tensor_copy(picked[:], table_words[g][:].bitcast(U32).indirect(offs_sb[:]))
-            picked_words.append(picked)
-            if g == 0:
-                nc.vector.tensor_copy(picked_scales[:], table_scales[:].indirect(offs_sb[:]))
-
-        def round_and_group(raw, label, on_scalar):
-            passes = raw.shape[1]
-            grouped = keep.tile([P, passes * P * PACK], BF16, name="grouped_" + label, tag="stage_" + label, align_bytes=64)
-            dst = grouped[:].rearrange("p (g c i t) -> p g c t i", g=passes, i=4, t=PACK)
-            src = raw.rearrange("p g t (c i) -> p g c t i", i=4)
-            if on_scalar:
-                nc.scalar.activation(dst[:, 0], src[:, 0], COPY)
-            else:
-                nc.vector.tensor_copy(dst, src)
+        def deal_columns(raw, label, copy):
+            grouped = keep.tile([P, H * PACK], BF16, name="grouped_" + label, tag="grouped_" + label, align_bytes=64)
+            copy(
+                grouped[:].rearrange("p (t m j) -> p m j t", t=PACK, j=PACK),
+                raw[:].rearrange("p j (m t) -> p m j t", t=PACK),
+            )
             return grouped
+
+        def scalar_copy(dst, src):
+            nc.scalar.activation(dst, src, COPY)
 
         def quantize(grouped, label):
             width = grouped.shape[1] // PACK
@@ -118,106 +99,111 @@ def tile_picked_ydiffex_gate_p_kernel(
             nc.vector.quantize_mx(out=codes[:].bitcast(FP8X4), scales=scales[:], in_=grouped[:])
             return codes, scales
 
-        def first_product(raw, label, b):
-            name = "%s%d" % (label, b)
-            if b == 0:
-                grouped = [round_and_group(raw[:, g : g + 1], "%s_%d" % (name, g), label == "z") for g in range(PASSES)]
-                quantized = [quantize(grouped[g], "%s_%d" % (name, g)) for g in range(PASSES)]
-                operands = [(codes[:], scales[:]) for codes, scales in quantized]
-            else:
-                codes, scales = quantize(round_and_group(raw[:], name, False), name)
-                operands = [(codes[:, g * P : (g + 1) * P], scales[:, g * P : (g + 1) * P]) for g in range(PASSES)]
-            acc = psum.tile([P, S], F32, name="acc_" + name, tag="acc_" + label)
-            for g in range(PASSES):
+        picked_words = []
+        picked_scales = keep.tile([P, S], U8, name="picked_scales", align_bytes=64)
+
+        def pick_words(g):
+            picked = keep.tile([P, S], U32, name="picked_words%d" % g, align_bytes=64)
+            nc.vector.tensor_copy(picked[:], table_words[g][:].bitcast(U32).indirect(offs_sb[:]))
+            picked_words.append(picked)
+
+        def first_product_pass(accs, quantized, g):
+            codes, scales = quantized
+            for t in range(PACK):
                 nc.tensor.matmul_mx(
-                    out=acc[:],
-                    lhsT=operands[g][0].bitcast(FP8X4),
-                    lhsT_scale=operands[g][1],
+                    out=accs[t][:],
+                    lhsT=codes[:, t * P : (t + 1) * P].bitcast(FP8X4),
+                    lhsT_scale=scales[:, t * P : (t + 1) * P],
                     rhs=picked_words[g][:].bitcast(FP8X4),
                     rhs_scale=picked_scales[4 * g : P, :],
                     start=(g == 0),
                     stop=(g == PASSES - 1),
                 )
-            return acc
 
-        def make_windows(b):
-            acc_z = first_product(raw_w2[b], "z", b)
-            nc.scalar.activation(windows["z", b][:, :S], acc_z[:], COPY)
-            acc_y = first_product(raw_w1[b], "y", b)
-            if b == 0:
-                nc.vector.tensor_copy(windows["y", b][:, :S], acc_y[:])
-                nc.vector.scalar_tensor_tensor(
-                    windows["q", b][:, :S], acc_y[:], -1.0, windows["z", b][:, :S], MULT, MULT
-                )
-            else:
-                nc.scalar.activation(windows["y", b][:, :S], acc_y[:], COPY)
-                nc.vector.scalar_tensor_tensor(
-                    windows["q", b][:, :S], acc_z[:], -1.0, windows["y", b][:, :S], MULT, MULT
-                )
+        acc_y = [psum.tile([P, S], F32, name="acc_y%d" % t, tag="bank%d" % t) for t in range(PACK)]
+        acc_z = [psum.tile([P, S], F32, name="acc_z%d" % t, tag="bank%d" % (PACK + t)) for t in range(PACK)]
 
-        unit_ps = psum_back.tile([P, PACK, P], F32, name="unit_ps", tag="back")
-        for t in range(PACK):
-            nc.tensor.matmul(
-                unit_ps[:, t, :], unit_sb[:, t : t + 1].to_broadcast([P, P]), ident[:],
-                start=True, stop=True, is_transpose=True,
-            )
-        unit_row = keep.tile([P, H], F32, name="unit_row")
-        nc.scalar.activation(
-            unit_row[:].rearrange("p (n t) -> p n t", t=PACK), unit_ps[:].rearrange("p t n -> p n t"), COPY
-        )
+        nc.vector.tensor_copy(picked_scales[:], table_scales[:].indirect(offs_sb[:]))
+        for g in range(PASSES):
+            grouped = deal_columns(raw_w1[g], "w1_%d" % g, (scalar_copy, nc.vector.tensor_copy)[g])
+            quantized = quantize(grouped, "w1_%d" % g)
+            pick_words(g)
+            first_product_pass(acc_y, quantized, g)
 
-        pieces = [(0, 512), (512, 256), (768, 256)]
-        hid_t = {r0: keep.tile([P, n // P, H], BF16, name="hid_t%d" % r0) for r0, n in pieces}
-
-        def fetch(label, b, r0, n):
-            fetched = ring.tile([P, n], F32, name="fetched_" + label, tag="fetched_" + label)
-            cols = slice(r0 // 16, (r0 + n) // 16)
-            nc.scalar.activation(fetched[:], windows[label, b][:].indirect(oth_sb[:, cols]), COPY)
+        def negated_other(t, h, tag):
+            fetched = keep.tile([P, HALF], F32, name="other", tag=tag, align_bytes=64)
+            cols = slice(h * HALF // 16, (h + 1) * HALF // 16)
+            nc.scalar.activation(fetched[:], windows["y", t][:].indirect(oth_sb[:, cols]), COPY, scale=-1.0)
             return fetched
 
-        def send(b, r0, n, gate, stage):
-            sender = keep.tile([P, n], F32, name="sender", tag="stage_" + stage, align_bytes=64)
-            cols = slice(r0 // 16, (r0 + n) // 16)
-            nc.vector.tensor_tensor(sender[:], windows["y", b][:].indirect(snd_sb[:, cols]), gate[:], MULT)
-            return sender
+        diff = {}
 
-        def add_up(b, r0, n, sender, other):
-            total = psum_sum.tile([P, n // P, P], F32, name="total", tag="total")
-            for c in range(n // P):
-                terms = (
-                    sender[:, c * P : (c + 1) * P],
-                    other[:, c * P : (c + 1) * P],
-                    old_sb[b][:, r0 + c * P : r0 + (c + 1) * P],
-                )
-                for k, term in enumerate(terms):
-                    nc.tensor.matmul(
-                        total[:, c, :], term, ident[:], start=(k == 0), stop=(k == len(terms) - 1), is_transpose=True
-                    )
-            return total
+        def difference(t, h, other, tag):
+            diff[t, h] = keep.tile([P, HALF], F32, name="diff", tag=tag, align_bytes=64)
+            cols = slice(h * HALF // 16, (h + 1) * HALF // 16)
+            nc.vector.tensor_tensor(diff[t, h][:], windows["y", t][:].indirect(snd_sb[:, cols]), other[:], ADD)
 
-        def scale_and_round(b, r0, n, total):
-            for p0, pn in pieces:
-                if r0 <= p0 < r0 + n:
-                    c0 = (p0 - r0) // P
-                    factor = unit_row[:, b * P : (b + 1) * P].unsqueeze(1).to_broadcast([P, pn // P, P])
-                    nc.vector.tensor_tensor(
-                        hid_t[p0][:, :, b * P : (b + 1) * P], total[:, c0 : c0 + pn // P, :], factor, MULT
-                    )
+        scalar_copy(windows["y", 0][:, :S], acc_y[0][:])
+        nc.vector.tensor_copy(windows["y", 1][:, :S], acc_y[1][:])
+        nc.vector.tensor_copy(windows["y", 2][:, :S], acc_y[2][:])
+        difference(0, 0, negated_other(0, 0, "other00"), "diff00")
+        grouped = deal_columns(raw_w2[0], "w2_0", nc.vector.tensor_copy)
+        difference(0, 1, negated_other(0, 1, "other01"), "raw_w2_0")
+        first_product_pass(acc_z, quantize(grouped, "w2_0"), 0)
+        difference(1, 0, negated_other(1, 0, "other10"), "grouped_w2_0")
+        difference(1, 1, negated_other(1, 1, "other11"), "diff11")
+        scalar_copy(windows["y", 3][:, :S], acc_y[3][:])
+        grouped = deal_columns(raw_w2[1], "w2_1", scalar_copy)
+        other = negated_other(2, 0, "raw_w2_1")
+        first_product_pass(acc_z, quantize(grouped, "w2_1"), 1)
+        difference(2, 0, other, "grouped_w2_1")
+        difference(2, 1, negated_other(2, 1, "other21"), "diff21")
+        grouped_w3 = keep.tile([P, N * PACK], BF16, name="grouped_w3", align_bytes=64)
+        nc.vector.tensor_copy(
+            grouped_w3[:].rearrange("p (c i j) -> p c j i", i=4, j=PACK),
+            raw_w3[:].rearrange("p j (c i) -> p c j i", i=4),
+        )
+        difference(3, 0, negated_other(3, 0, "other30"), "diff30")
+        w3_codes, w3_scales = quantize(grouped_w3, "w3")
+        difference(3, 1, negated_other(3, 1, "other31"), "diff31")
+        for t in range(PACK):
+            nc.scalar.activation(windows["z", t][:, :S], acc_z[t][:], COPY, scale=unit_sb[:, t : t + 1])
 
-        def last_product(r0, w3_codes, w3_scales, bank, copy):
-            p0 = max(start for start, n in pieces if start <= r0)
-            back = psum_back.tile([P, 2, 2, P], F32, name="back", tag="back")
-            for a in range(2):
-                words = hid_t[p0][:, (r0 - p0) // P + a, :].bitcast(F32)
-                for u in range(2):
-                    nc.tensor.transpose(back[:, a, u, :], words[:, u : H // 2 : 2], ident[:])
-            grouped = keep.tile([P, QUARTER * PACK], BF16, name="grouped_hid%d" % r0, align_bytes=64)
-            copy(
-                grouped[:].bitcast(F32).rearrange("p (a r u) -> p a r u", a=2, u=2),
-                back[:].rearrange("p a u r -> p a r u"),
+        chunks = [(0, 512), (512, 256), (768, 128), (896, 128)]
+        gates = {}
+        for h in range(2):
+            for t in range(FUSED_PLANES, PACK):
+                gates[t, h] = keep.tile([P, HALF], F32, name="gate%d_%d" % (t, h))
+                cols = slice(h * HALF // 16, (h + 1) * HALF // 16)
+                scalar_copy(gates[t, h][:], windows["z", t][:].indirect(oth_sb[:, cols]))
+
+        def weighted(r0, n, t):
+            h, c0 = divmod(r0, HALF)
+            wex = ring.tile([P, n], F32, name="wex", tag="wex")
+            if t < FUSED_PLANES:
+                gate = windows["z", t][:].indirect(oth_sb[:, r0 // 16 : (r0 + n) // 16])
+            else:
+                gate = gates[t, h][:, c0 : c0 + n]
+            nc.vector.tensor_tensor(wex[:], gate, diff[t, h][:, c0 : c0 + n], MULT)
+            return wex
+
+        def hidden(r0, n, t, wex, planes):
+            h, c0 = divmod(r0, HALF)
+            nc.vector.scalar_tensor_tensor(
+                planes[:, t, :], old_sb[h][:, t, c0 : c0 + n], unit_sb[:, t : t + 1], wex[:], MULT, ADD
             )
+
+        def group_hidden(r0, n, planes):
+            grouped = keep.tile([P, n * PACK], BF16, name="grouped_hid%d" % r0, align_bytes=64)
+            nc.scalar.copy(
+                grouped[:].rearrange("p (c i t) -> p c t i", i=4, t=PACK),
+                planes[:].rearrange("p t (c i) -> p c t i", i=4),
+            )
+            return grouped
+
+        def last_product(r0, n, grouped, bank):
             codes, scales = quantize(grouped, "hid%d" % r0)
-            acc = psum.tile([P, QUARTER], F32, name="acc_out", tag=bank)
+            acc = psum.tile([P, n], F32, name="acc_out", tag="bank%d" % bank)
             nc.tensor.matmul_mx(
                 out=acc[:],
                 lhsT=w3_codes[:].bitcast(FP8X4),
@@ -227,26 +213,19 @@ def tile_picked_ydiffex_gate_p_kernel(
                 start=True,
                 stop=True,
             )
-            result = keep.tile([P, QUARTER], F32, name="result%d" % r0)
-            copy(result[:], acc[:])
-            nc.sync.dma_start(out[:, r0 : r0 + QUARTER], result[:])
+            result = keep.tile([P, n], F32, name="result%d" % r0)
+            nc.scalar.copy(result[:], acc[:])
+            nc.sync.dma_start(out[:, r0 : r0 + n], result[:])
 
-        make_windows(0)
-        for b in range(BLOCKS - 1):
-            gates = [fetch("z", b, r0, 512) for r0 in (0, 512)]
-            others = [fetch("q", b, r0, 512) for r0 in (0, 512)]
-            make_windows(b + 1)
-            for h, label in enumerate(("z", "y")):
-                sender = send(b, 512 * h, 512, gates[h], "%s%d" % (label, b + 1))
-                scale_and_round(b, 512 * h, 512, add_up(b, 512 * h, 512, sender, others[h]))
-        w3_codes, w3_scales = quantize(round_and_group(raw_w3[:], "w3", False), "w3")
-        last = BLOCKS - 1
-        for r0, n in pieces:
-            gate = fetch("z", last, r0, n)
-            other = fetch("q", last, r0, n)
-            sender = send(last, r0, n, gate, "last%d" % r0)
-            scale_and_round(last, r0, n, add_up(last, r0, n, sender, other))
-        last_product(0, w3_codes, w3_scales, "acc_z", nc.vector.tensor_copy)
-        last_product(256, w3_codes, w3_scales, "acc_y", nc.vector.tensor_copy)
-        last_product(512, w3_codes, w3_scales, "acc_z", nc.scalar.copy)
-        last_product(768, w3_codes, w3_scales, "acc_y", nc.scalar.copy)
+        waiting = None
+        for index, (r0, n) in enumerate(chunks):
+            planes = keep.tile([P, PACK, n], BF16, name="planes%d" % r0)
+            wex = {0: weighted(r0, n, 0)}
+            for t in range(PACK):
+                if t + 1 < PACK:
+                    wex[t + 1] = weighted(r0, n, t + 1)
+                hidden(r0, n, t, wex[t], planes)
+            if waiting is not None:
+                last_product(*waiting)
+            waiting = (r0, n, group_hidden(r0, n, planes), index % PACK)
+        last_product(*waiting)

@@ -21,7 +21,6 @@ PACK = 4
 PASSES = K // (P * PACK)
 SPARE = 32
 HALF = U // 2
-FUSED_PLANES = 2
 
 
 def tile_picked_ydiffex_gate_p_kernel(
@@ -30,7 +29,6 @@ def tile_picked_ydiffex_gate_p_kernel(
     nc = tc.nc
     with ExitStack() as ctx:
         keep = ctx.enter_context(tc.tile_pool(name="keep", bufs=1))
-        ring = ctx.enter_context(tc.tile_pool(name="ring", bufs=3))
         psum = ctx.enter_context(tc.psum_pool(name="psum", bufs=1))
 
         offs_sb = keep.tile([P, S // 16], U16, name="offs_sb")
@@ -40,6 +38,11 @@ def tile_picked_ydiffex_gate_p_kernel(
 
         table_scales = keep.tile([P, T], U8, name="table_scales", align_bytes=64)
         nc.gpsimd.memset(table_scales[:].bitcast(I32), 0)
+        for quad in range(4):
+            nc.gpsimd.dma_start(
+                table_scales[32 * quad : 32 * quad + 4 * PASSES, :].bitcast(I32),
+                x_scales[:, 4 * quad : 4 * quad + 4, :].bitcast(I32),
+            )
 
         def load_words(g):
             words = keep.tile([P, T], I32, name="table_words%d" % g, align_bytes=64)
@@ -55,22 +58,17 @@ def tile_picked_ydiffex_gate_p_kernel(
         raw_w1, table_words = [], []
         for g in range(PASSES):
             raw_w1.append(load_rows(w1, g, "w1_%d" % g))
-            if g == 0:
-                for quad in range(4):
-                    nc.sync.dma_start(
-                        table_scales[32 * quad : 32 * quad + 4 * PASSES, :].bitcast(I32),
-                        x_scales[:, 4 * quad : 4 * quad + 4, :].bitcast(I32),
-                    )
             table_words.append(load_words(g))
         nc.sync.dma_start(oth_sb[:], oth)
         nc.sync.dma_start(snd_sb[:], snd)
         raw_w2 = [load_rows(w2, g, "w2_%d" % g) for g in range(PASSES)]
         unit_sb = keep.tile([P, PACK], F32, name="unit_sb")
         nc.sync.dma_start(unit_sb[:], unit.rearrange("(p t) o -> p (t o)", t=PACK))
+        old_rows = old.rearrange("(p t) r -> p t r", t=PACK)
         old_sb = []
-        for h in range(2):
-            kept = keep.tile([P, PACK, HALF], F32, name="old%d" % h)
-            nc.sync.dma_start(kept[:], old[:, h * HALF : (h + 1) * HALF].rearrange("(p t) r -> p t r", t=PACK))
+        for pair in range(2):
+            kept = keep.tile([P, 2, U], F32, name="old%d" % pair)
+            nc.sync.dma_start(kept[:], old_rows[:, 2 * pair : 2 * pair + 2, :])
             old_sb.append(kept)
         raw_w3 = load_rows(w3, 0, "w3")
 
@@ -78,15 +76,16 @@ def tile_picked_ydiffex_gate_p_kernel(
         for label in ("y", "z"):
             for t in range(PACK):
                 window = keep.tile([P, S + SPARE], F32, name="window_%s%d" % (label, t))
-                nc.gpsimd.memset(window[:, S:], 0.0)
+                nc.vector.memset(window[:, S:], 0.0)
                 windows[label, t] = window
 
-        def deal_columns(raw, label, copy):
-            grouped = keep.tile([P, H * PACK], BF16, name="grouped_" + label, tag="grouped_" + label, align_bytes=64)
-            copy(
-                grouped[:].rearrange("p (t m j) -> p m j t", t=PACK, j=PACK),
-                raw[:].rearrange("p j (m t) -> p m j t", t=PACK),
-            )
+        def deal_columns(raw, tag, *copies):
+            grouped = keep.tile([P, H * PACK], BF16, name="grouped", tag=tag, align_bytes=64)
+            dst = grouped[:].rearrange("p (t m j) -> p m j t", t=PACK, j=PACK)
+            src = raw[:].rearrange("p j (m t) -> p m j t", t=PACK)
+            share = P // len(copies)
+            for index, copy in enumerate(copies):
+                copy(dst[:, index * share : (index + 1) * share], src[:, index * share : (index + 1) * share])
             return grouped
 
         def scalar_copy(dst, src):
@@ -94,13 +93,12 @@ def tile_picked_ydiffex_gate_p_kernel(
 
         def quantize(grouped, label):
             width = grouped.shape[1] // PACK
-            codes = keep.tile([P, width], U32, name="codes_" + label, align_bytes=64)
-            scales = keep.tile([P, width], U8, name="scales_" + label, align_bytes=64)
+            codes = keep.tile([P, width], U32, name="codes_" + label, tag="codes_" + label, align_bytes=64)
+            scales = keep.tile([P, width], U8, name="scales_" + label, tag="scales_" + label, align_bytes=64)
             nc.vector.quantize_mx(out=codes[:].bitcast(FP8X4), scales=scales[:], in_=grouped[:])
             return codes, scales
 
         picked_words = []
-        picked_scales = keep.tile([P, S], U8, name="picked_scales", align_bytes=64)
 
         def pick_words(g):
             picked = keep.tile([P, S], U32, name="picked_words%d" % g, align_bytes=64)
@@ -123,85 +121,93 @@ def tile_picked_ydiffex_gate_p_kernel(
         acc_y = [psum.tile([P, S], F32, name="acc_y%d" % t, tag="bank%d" % t) for t in range(PACK)]
         acc_z = [psum.tile([P, S], F32, name="acc_z%d" % t, tag="bank%d" % (PACK + t)) for t in range(PACK)]
 
+        pick_words(0)
+        quantized = quantize(deal_columns(raw_w1[0], "w1_0", scalar_copy), "w1_0")
+        picked_scales = keep.tile([P, S], U8, name="picked_scales", tag="w1_0", align_bytes=64)
         nc.vector.tensor_copy(picked_scales[:], table_scales[:].indirect(offs_sb[:]))
-        for g in range(PASSES):
-            grouped = deal_columns(raw_w1[g], "w1_%d" % g, (scalar_copy, nc.vector.tensor_copy)[g])
-            quantized = quantize(grouped, "w1_%d" % g)
-            pick_words(g)
-            first_product_pass(acc_y, quantized, g)
+        first_product_pass(acc_y, quantized, 0)
+        quantized = quantize(deal_columns(raw_w1[1], "w1_1", nc.vector.tensor_copy, scalar_copy), "w1_1")
+        pick_words(1)
+        first_product_pass(acc_y, quantized, 1)
 
-        def negated_other(t, h, tag):
-            fetched = keep.tile([P, HALF], F32, name="other", tag=tag, align_bytes=64)
+        def negated_other(t, h, fetched):
             cols = slice(h * HALF // 16, (h + 1) * HALF // 16)
-            nc.scalar.activation(fetched[:], windows["y", t][:].indirect(oth_sb[:, cols]), COPY, scale=-1.0)
+            nc.scalar.activation(fetched, windows["y", t][:].indirect(oth_sb[:, cols]), COPY, scale=-1.0)
             return fetched
 
-        diff = {}
+        def stage(tag, width=HALF):
+            return keep.tile([P, width], F32, name="stage", tag=tag, align_bytes=64)[:]
 
-        def difference(t, h, other, tag):
-            diff[t, h] = keep.tile([P, HALF], F32, name="diff", tag=tag, align_bytes=64)
+        diff_first = {}
+
+        def difference(t, h, other, tag=None):
+            if h == 0:
+                diff_first[t] = keep.tile([P, HALF], F32, name="diff", tag=tag, align_bytes=64)
+                dst = diff_first[t][:]
+            else:
+                dst = diff_second[:, t, :]
             cols = slice(h * HALF // 16, (h + 1) * HALF // 16)
-            nc.vector.tensor_tensor(diff[t, h][:], windows["y", t][:].indirect(snd_sb[:, cols]), other[:], ADD)
+            nc.vector.tensor_tensor(dst, windows["y", t][:].indirect(snd_sb[:, cols]), other, ADD)
 
         scalar_copy(windows["y", 0][:, :S], acc_y[0][:])
         nc.vector.tensor_copy(windows["y", 1][:, :S], acc_y[1][:])
         nc.vector.tensor_copy(windows["y", 2][:, :S], acc_y[2][:])
-        difference(0, 0, negated_other(0, 0, "other00"), "diff00")
-        grouped = deal_columns(raw_w2[0], "w2_0", nc.vector.tensor_copy)
-        difference(0, 1, negated_other(0, 1, "other01"), "raw_w2_0")
+        difference(0, 0, negated_other(0, 0, stage("other00")), "diff00")
+        grouped = deal_columns(raw_w2[0], "other00", nc.vector.tensor_copy)
+        difference(1, 0, negated_other(1, 0, stage("other10")), "raw_w2_0")
         first_product_pass(acc_z, quantize(grouped, "w2_0"), 0)
-        difference(1, 0, negated_other(1, 0, "other10"), "grouped_w2_0")
-        difference(1, 1, negated_other(1, 1, "other11"), "diff11")
+        diff_second = keep.tile([P, PACK, HALF], F32, name="diff_second", tag="other00", align_bytes=64)
+        difference(0, 1, negated_other(0, 1, stage("other01")))
+        difference(1, 1, negated_other(1, 1, stage("other11")))
         scalar_copy(windows["y", 3][:, :S], acc_y[3][:])
-        grouped = deal_columns(raw_w2[1], "w2_1", scalar_copy)
-        other = negated_other(2, 0, "raw_w2_1")
+        grouped = deal_columns(raw_w2[1], "other10", scalar_copy)
+        late = stage("raw_w2_1", 3 * HALF)
+        other = negated_other(2, 0, late[:, :HALF])
         first_product_pass(acc_z, quantize(grouped, "w2_1"), 1)
-        difference(2, 0, other, "grouped_w2_1")
-        difference(2, 1, negated_other(2, 1, "other21"), "diff21")
-        grouped_w3 = keep.tile([P, N * PACK], BF16, name="grouped_w3", align_bytes=64)
-        nc.vector.tensor_copy(
+        difference(2, 0, other, "other10")
+        difference(2, 1, negated_other(2, 1, late[:, HALF : 2 * HALF]))
+        difference(3, 1, negated_other(3, 1, late[:, 2 * HALF :]))
+        for t in range(PACK):
+            nc.scalar.activation(windows["z", t][:, :S], acc_z[t][:], COPY, scale=unit_sb[:, t : t + 1])
+        other = negated_other(3, 0, stage("codes_w2_1"))
+
+        wex_first = keep.tile([P, PACK, HALF], F32, name="wex_first")
+        for t in range(PACK):
+            if t == PACK - 1:
+                difference(3, 0, other, "diff30")
+            gate = windows["z", t][:].indirect(oth_sb[:, : HALF // 16])
+            nc.vector.tensor_tensor(wex_first[:, t, :], gate, diff_first[t][:], MULT)
+
+        scaled_old = keep.tile([P, PACK, U], F32, name="scaled_old", tag="scales_w2_1", align_bytes=64)
+        for t in range(PACK):
+            nc.scalar.activation(scaled_old[:, t, :], old_sb[t // 2][:, t % 2, :], COPY, scale=unit_sb[:, t : t + 1])
+
+        grouped_w3 = keep.tile([P, N * PACK], BF16, name="grouped_w3", tag="codes_w2_1", align_bytes=64)
+        scalar_copy(
             grouped_w3[:].rearrange("p (c i j) -> p c j i", i=4, j=PACK),
             raw_w3[:].rearrange("p j (c i) -> p c j i", i=4),
         )
-        difference(3, 0, negated_other(3, 0, "other30"), "diff30")
         w3_codes, w3_scales = quantize(grouped_w3, "w3")
-        difference(3, 1, negated_other(3, 1, "other31"), "diff31")
-        for t in range(PACK):
-            nc.scalar.activation(windows["z", t][:, :S], acc_z[t][:], COPY, scale=unit_sb[:, t : t + 1])
 
-        chunks = [(0, 512), (512, 256), (768, 128), (896, 128)]
-        gates = {}
-        for h in range(2):
-            for t in range(FUSED_PLANES, PACK):
-                gates[t, h] = keep.tile([P, HALF], F32, name="gate%d_%d" % (t, h))
-                cols = slice(h * HALF // 16, (h + 1) * HALF // 16)
-                scalar_copy(gates[t, h][:], windows["z", t][:].indirect(oth_sb[:, cols]))
+        def fetch_gates(r0, n):
+            gates = keep.tile([P, PACK, n], F32, name="gates%d" % r0)
+            for t in range(PACK):
+                scalar_copy(gates[:, t, :], windows["z", t][:].indirect(oth_sb[:, r0 // 16 : (r0 + n) // 16]))
+            return gates
 
-        def weighted(r0, n, t):
-            h, c0 = divmod(r0, HALF)
-            wex = ring.tile([P, n], F32, name="wex", tag="wex")
-            if t < FUSED_PLANES:
-                gate = windows["z", t][:].indirect(oth_sb[:, r0 // 16 : (r0 + n) // 16])
-            else:
-                gate = gates[t, h][:, c0 : c0 + n]
-            nc.vector.tensor_tensor(wex[:], gate, diff[t, h][:, c0 : c0 + n], MULT)
+        def weigh(r0, n, gates):
+            wex = keep.tile([P, PACK, n], F32, name="wex%d" % r0)
+            nc.vector.tensor_tensor(wex[:], gates[:], diff_second[:, :, r0 - HALF : r0 - HALF + n], MULT)
             return wex
 
-        def hidden(r0, n, t, wex, planes):
-            h, c0 = divmod(r0, HALF)
-            nc.vector.scalar_tensor_tensor(
-                planes[:, t, :], old_sb[h][:, t, c0 : c0 + n], unit_sb[:, t : t + 1], wex[:], MULT, ADD
-            )
-
-        def group_hidden(r0, n, planes):
+        def last_product(r0, n, wex, bank, copy):
             grouped = keep.tile([P, n * PACK], BF16, name="grouped_hid%d" % r0, align_bytes=64)
-            nc.scalar.copy(
+            nc.vector.tensor_tensor(
                 grouped[:].rearrange("p (c i t) -> p c t i", i=4, t=PACK),
-                planes[:].rearrange("p t (c i) -> p c t i", i=4),
+                wex[:].rearrange("p t (c i) -> p c t i", i=4),
+                scaled_old[:, :, r0 : r0 + n].rearrange("p t (c i) -> p c t i", i=4),
+                ADD,
             )
-            return grouped
-
-        def last_product(r0, n, grouped, bank):
             codes, scales = quantize(grouped, "hid%d" % r0)
             acc = psum.tile([P, n], F32, name="acc_out", tag="bank%d" % bank)
             nc.tensor.matmul_mx(
@@ -214,18 +220,16 @@ def tile_picked_ydiffex_gate_p_kernel(
                 stop=True,
             )
             result = keep.tile([P, n], F32, name="result%d" % r0)
-            nc.scalar.copy(result[:], acc[:])
+            copy(result[:], acc[:])
             nc.sync.dma_start(out[:, r0 : r0 + n], result[:])
 
-        waiting = None
+        wex_last = keep.tile([P, PACK, 128], F32, name="wex_last")
+        for t in range(PACK):
+            gate = windows["z", t][:].indirect(oth_sb[:, 896 // 16 :])
+            nc.vector.tensor_tensor(wex_last[:, t, :], gate, diff_second[:, t, 896 - HALF :], MULT)
+        chunks = [(512, 256), (768, 128)]
+        gates = [fetch_gates(r0, n) for r0, n in chunks]
+        last_product(0, HALF, wex_first, 0, nc.scalar.copy)
         for index, (r0, n) in enumerate(chunks):
-            planes = keep.tile([P, PACK, n], BF16, name="planes%d" % r0)
-            wex = {0: weighted(r0, n, 0)}
-            for t in range(PACK):
-                if t + 1 < PACK:
-                    wex[t + 1] = weighted(r0, n, t + 1)
-                hidden(r0, n, t, wex[t], planes)
-            if waiting is not None:
-                last_product(*waiting)
-            waiting = (r0, n, group_hidden(r0, n, planes), index % PACK)
-        last_product(*waiting)
+            last_product(r0, n, weigh(r0, n, gates[index]), index + 1, nc.scalar.copy)
+        last_product(896, 128, wex_last, 3, nc.vector.tensor_copy)

@@ -19,8 +19,12 @@ COPY = mybir.ActivationFunctionType.Copy
 P = 128
 PACK = 4
 PASSES = K // (P * PACK)
+PER_COLUMN = 16
+LINE = 4
 SPARE = 32
 HALF = U // 2
+SCALAR_CHUNKS = [(512, 256), (768, 128)]
+LAST_START, LAST_WIDTH = 896, 128
 
 
 def tile_picked_ydiffex_gate_p_kernel(
@@ -31,9 +35,12 @@ def tile_picked_ydiffex_gate_p_kernel(
         keep = ctx.enter_context(tc.tile_pool(name="keep", bufs=1))
         psum = ctx.enter_context(tc.psum_pool(name="psum", bufs=1))
 
-        offs_sb = keep.tile([P, S // 16], U16, name="offs_sb")
-        snd_sb = keep.tile([P, U // 16], U16, name="snd_sb")
-        oth_sb = keep.tile([P, U // 16], U16, name="oth_sb")
+        def entries(list_tile, start, count):
+            return list_tile[:, start // PER_COLUMN : (start + count) // PER_COLUMN]
+
+        offs_sb = keep.tile([P, S // PER_COLUMN], U16, name="offs_sb")
+        snd_sb = keep.tile([P, U // PER_COLUMN], U16, name="snd_sb")
+        oth_sb = keep.tile([P, U // PER_COLUMN], U16, name="oth_sb")
         nc.sync.dma_start(offs_sb[:], offs)
 
         table_scales = keep.tile([P, T], U8, name="table_scales", align_bytes=64)
@@ -66,7 +73,7 @@ def tile_picked_ydiffex_gate_p_kernel(
         nc.sync.dma_start(unit_sb[:], unit.rearrange("(p t) o -> p (t o)", t=PACK))
         old_rows = old.rearrange("(p t) r -> p t r", t=PACK)
         old_sb = []
-        for pair in range(2):
+        for pair in range(PACK // 2):
             kept = keep.tile([P, 2, U], F32, name="old%d" % pair)
             nc.sync.dma_start(kept[:], old_rows[:, 2 * pair : 2 * pair + 2, :])
             old_sb.append(kept)
@@ -100,83 +107,89 @@ def tile_picked_ydiffex_gate_p_kernel(
 
         picked_words = []
 
-        def pick_words(g):
+        def pick_words(g, parts):
             picked = keep.tile([P, S], U32, name="picked_words%d" % g, align_bytes=64)
-            nc.vector.tensor_copy(picked[:], table_words[g][:].bitcast(U32).indirect(offs_sb[:]))
+            width = S // parts
+            for start in range(0, S, width):
+                window = table_words[g][:].bitcast(U32)
+                nc.vector.tensor_copy(picked[:, start : start + width], window.indirect(entries(offs_sb, start, width)))
             picked_words.append(picked)
 
-        def first_product_pass(accs, quantized, g):
+        whole_planes = [(t, 0, S) for t in range(PACK)]
+
+        def first_product_pass(accs, quantized, g, steps):
             codes, scales = quantized
-            for t in range(PACK):
+            for t, lo, hi in steps:
                 nc.tensor.matmul_mx(
-                    out=accs[t][:],
+                    out=accs[t][:, lo:hi],
                     lhsT=codes[:, t * P : (t + 1) * P].bitcast(FP8X4),
                     lhsT_scale=scales[:, t * P : (t + 1) * P],
-                    rhs=picked_words[g][:].bitcast(FP8X4),
-                    rhs_scale=picked_scales[4 * g : P, :],
+                    rhs=picked_words[g][:, lo:hi].bitcast(FP8X4),
+                    rhs_scale=picked_scales[4 * g : P, lo:hi],
                     start=(g == 0),
-                    stop=(g == PASSES - 1),
+                    stop=(g == PASSES - 1 and hi == S),
                 )
 
         acc_y = [psum.tile([P, S], F32, name="acc_y%d" % t, tag="bank%d" % t) for t in range(PACK)]
         acc_z = [psum.tile([P, S], F32, name="acc_z%d" % t, tag="bank%d" % (PACK + t)) for t in range(PACK)]
 
-        pick_words(0)
+        pick_words(0, 1)
         quantized = quantize(deal_columns(raw_w1[0], "w1_0", scalar_copy), "w1_0")
         picked_scales = keep.tile([P, S], U8, name="picked_scales", tag="w1_0", align_bytes=64)
         nc.vector.tensor_copy(picked_scales[:], table_scales[:].indirect(offs_sb[:]))
-        first_product_pass(acc_y, quantized, 0)
+        first_product_pass(acc_y, quantized, 0, whole_planes)
         quantized = quantize(deal_columns(raw_w1[1], "w1_1", nc.vector.tensor_copy, scalar_copy), "w1_1")
-        pick_words(1)
-        first_product_pass(acc_y, quantized, 1)
+        pick_words(1, 2)
+        halves = [(t, lo, lo + S // 2) for lo in (0, S // 2) for t in range(2)]
+        first_product_pass(acc_y, quantized, 1, halves + whole_planes[2:])
 
         def negated_other(t, h, fetched):
-            cols = slice(h * HALF // 16, (h + 1) * HALF // 16)
-            nc.scalar.activation(fetched, windows["y", t][:].indirect(oth_sb[:, cols]), COPY, scale=-1.0)
+            window = windows["y", t][:]
+            nc.scalar.activation(fetched, window.indirect(entries(oth_sb, h * HALF, HALF)), COPY, scale=-1.0)
             return fetched
 
         def stage(tag, width=HALF):
             return keep.tile([P, width], F32, name="stage", tag=tag, align_bytes=64)[:]
 
+        def difference(dst, t, h, negated):
+            window = windows["y", t][:]
+            nc.vector.tensor_tensor(dst, window.indirect(entries(snd_sb, h * HALF, HALF)), negated, ADD)
+
         diff_first = {}
 
-        def difference(t, h, other, tag=None):
-            if h == 0:
-                diff_first[t] = keep.tile([P, HALF], F32, name="diff", tag=tag, align_bytes=64)
-                dst = diff_first[t][:]
-            else:
-                dst = diff_second[:, t, :]
-            cols = slice(h * HALF // 16, (h + 1) * HALF // 16)
-            nc.vector.tensor_tensor(dst, windows["y", t][:].indirect(snd_sb[:, cols]), other, ADD)
+        def first_difference(t, negated, tag):
+            diff_first[t] = stage(tag)
+            difference(diff_first[t], t, 0, negated)
 
         scalar_copy(windows["y", 0][:, :S], acc_y[0][:])
-        nc.vector.tensor_copy(windows["y", 1][:, :S], acc_y[1][:])
-        nc.vector.tensor_copy(windows["y", 2][:, :S], acc_y[2][:])
-        difference(0, 0, negated_other(0, 0, stage("other00")), "diff00")
+        for t in (1, 2, 3):
+            nc.vector.tensor_copy(windows["y", t][:, :S], acc_y[t][:])
+        first_difference(0, negated_other(0, 0, stage("other00")), "diff00")
         grouped = deal_columns(raw_w2[0], "other00", nc.vector.tensor_copy)
-        difference(1, 0, negated_other(1, 0, stage("other10")), "raw_w2_0")
-        first_product_pass(acc_z, quantize(grouped, "w2_0"), 0)
+        first_difference(1, negated_other(1, 0, stage("other10")), "raw_w2_0")
+        first_product_pass(acc_z, quantize(grouped, "w2_0"), 0, whole_planes)
         diff_second = keep.tile([P, PACK, HALF], F32, name="diff_second", tag="other00", align_bytes=64)
-        difference(0, 1, negated_other(0, 1, stage("other01")))
-        difference(1, 1, negated_other(1, 1, stage("other11")))
-        scalar_copy(windows["y", 3][:, :S], acc_y[3][:])
+        difference(diff_second[:, 0, :], 0, 1, negated_other(0, 1, stage("other01")))
+        difference(diff_second[:, 1, :], 1, 1, negated_other(1, 1, stage("other11")))
         grouped = deal_columns(raw_w2[1], "other10", scalar_copy)
         late = stage("raw_w2_1", 3 * HALF)
-        other = negated_other(2, 0, late[:, :HALF])
-        first_product_pass(acc_z, quantize(grouped, "w2_1"), 1)
-        difference(2, 0, other, "other10")
-        difference(2, 1, negated_other(2, 1, late[:, HALF : 2 * HALF]))
-        difference(3, 1, negated_other(3, 1, late[:, 2 * HALF :]))
+        negated = negated_other(2, 0, late[:, :HALF])
+        first_product_pass(acc_z, quantize(grouped, "w2_1"), 1, whole_planes)
+        first_difference(2, negated, "other10")
+        difference(diff_second[:, 2, :], 2, 1, negated_other(2, 1, late[:, HALF : 2 * HALF]))
+        difference(diff_second[:, 3, :], 3, 1, negated_other(3, 1, late[:, 2 * HALF :]))
         for t in range(PACK):
             nc.scalar.activation(windows["z", t][:, :S], acc_z[t][:], COPY, scale=unit_sb[:, t : t + 1])
-        other = negated_other(3, 0, stage("codes_w2_1"))
+        negated = negated_other(3, 0, stage("codes_w2_1"))
+
+        def weigh_fused(dst, t, r0, n, diff):
+            nc.vector.tensor_tensor(dst, windows["z", t][:].indirect(entries(oth_sb, r0, n)), diff, MULT)
 
         wex_first = keep.tile([P, PACK, HALF], F32, name="wex_first")
-        for t in range(PACK):
-            if t == PACK - 1:
-                difference(3, 0, other, "diff30")
-            gate = windows["z", t][:].indirect(oth_sb[:, : HALF // 16])
-            nc.vector.tensor_tensor(wex_first[:, t, :], gate, diff_first[t][:], MULT)
+        for t in range(PACK - 1):
+            weigh_fused(wex_first[:, t, :], t, 0, HALF, diff_first[t])
+        first_difference(3, negated, "diff30")
+        weigh_fused(wex_first[:, 3, :], 3, 0, HALF, diff_first[3])
 
         scaled_old = keep.tile([P, PACK, U], F32, name="scaled_old", tag="scales_w2_1", align_bytes=64)
         for t in range(PACK):
@@ -184,31 +197,31 @@ def tile_picked_ydiffex_gate_p_kernel(
 
         grouped_w3 = keep.tile([P, N * PACK], BF16, name="grouped_w3", tag="codes_w2_1", align_bytes=64)
         scalar_copy(
-            grouped_w3[:].rearrange("p (c i j) -> p c j i", i=4, j=PACK),
-            raw_w3[:].rearrange("p j (c i) -> p c j i", i=4),
+            grouped_w3[:].rearrange("p (c i j) -> p c j i", i=LINE, j=PACK),
+            raw_w3[:].rearrange("p j (c i) -> p c j i", i=LINE),
         )
         w3_codes, w3_scales = quantize(grouped_w3, "w3")
 
         def fetch_gates(r0, n):
             gates = keep.tile([P, PACK, n], F32, name="gates%d" % r0)
             for t in range(PACK):
-                scalar_copy(gates[:, t, :], windows["z", t][:].indirect(oth_sb[:, r0 // 16 : (r0 + n) // 16]))
+                scalar_copy(gates[:, t, :], windows["z", t][:].indirect(entries(oth_sb, r0, n)))
             return gates
 
-        def weigh(r0, n, gates):
+        def weigh_fetched(r0, n, gates):
             wex = keep.tile([P, PACK, n], F32, name="wex%d" % r0)
             nc.vector.tensor_tensor(wex[:], gates[:], diff_second[:, :, r0 - HALF : r0 - HALF + n], MULT)
             return wex
 
-        def last_product(r0, n, wex, bank, copy):
-            grouped = keep.tile([P, n * PACK], BF16, name="grouped_hid%d" % r0, align_bytes=64)
+        def last_product(r0, n, wex, bank, copy_out):
+            grouped_hid = keep.tile([P, n * PACK], BF16, name="grouped_hid%d" % r0, align_bytes=64)
             nc.vector.tensor_tensor(
-                grouped[:].rearrange("p (c i t) -> p c t i", i=4, t=PACK),
-                wex[:].rearrange("p t (c i) -> p c t i", i=4),
-                scaled_old[:, :, r0 : r0 + n].rearrange("p t (c i) -> p c t i", i=4),
+                grouped_hid[:].rearrange("p (c i t) -> p c t i", i=LINE, t=PACK),
+                wex[:].rearrange("p t (c i) -> p c t i", i=LINE),
+                scaled_old[:, :, r0 : r0 + n].rearrange("p t (c i) -> p c t i", i=LINE),
                 ADD,
             )
-            codes, scales = quantize(grouped, "hid%d" % r0)
+            codes, scales = quantize(grouped_hid, "hid%d" % r0)
             acc = psum.tile([P, n], F32, name="acc_out", tag="bank%d" % bank)
             nc.tensor.matmul_mx(
                 out=acc[:],
@@ -220,16 +233,15 @@ def tile_picked_ydiffex_gate_p_kernel(
                 stop=True,
             )
             result = keep.tile([P, n], F32, name="result%d" % r0)
-            copy(result[:], acc[:])
+            copy_out(result[:], acc[:])
             nc.sync.dma_start(out[:, r0 : r0 + n], result[:])
 
-        wex_last = keep.tile([P, PACK, 128], F32, name="wex_last")
+        wex_last = keep.tile([P, PACK, LAST_WIDTH], F32, name="wex_last")
         for t in range(PACK):
-            gate = windows["z", t][:].indirect(oth_sb[:, 896 // 16 :])
-            nc.vector.tensor_tensor(wex_last[:, t, :], gate, diff_second[:, t, 896 - HALF :], MULT)
-        chunks = [(512, 256), (768, 128)]
-        gates = [fetch_gates(r0, n) for r0, n in chunks]
+            weigh_fused(wex_last[:, t, :], t, LAST_START, LAST_WIDTH, diff_second[:, t, LAST_START - HALF :])
+        fetched_gates = [fetch_gates(r0, n) for r0, n in SCALAR_CHUNKS]
+
         last_product(0, HALF, wex_first, 0, nc.scalar.copy)
-        for index, (r0, n) in enumerate(chunks):
-            last_product(r0, n, weigh(r0, n, gates[index]), index + 1, nc.scalar.copy)
-        last_product(896, 128, wex_last, 3, nc.vector.tensor_copy)
+        for index, (r0, n) in enumerate(SCALAR_CHUNKS):
+            last_product(r0, n, weigh_fetched(r0, n, fetched_gates[index]), index + 1, nc.scalar.copy)
+        last_product(LAST_START, LAST_WIDTH, wex_last, PACK - 1, nc.vector.tensor_copy)

from contextlib import ExitStack

import concourse.mybir as mybir

K, T, S, N, H, U = 1024, 2048, 512, 128, 512, 1024
FLOPS = 2 * (2 * K * H * S) + 2 * H * N * U

F32 = mybir.dt.float32
BF16 = mybir.dt.bfloat16
I32 = mybir.dt.int32
U32 = mybir.dt.uint32
U16 = mybir.dt.uint16
U8 = mybir.dt.uint8
FP8X4 = mybir.dt.float8_e4m3fn_x4
MULT = mybir.AluOpType.mult
ADD = mybir.AluOpType.add
COPY = mybir.ActivationFunctionType.Copy

P = 128
PACK = 4
PASSES = K // (P * PACK)
PER_COLUMN = 16
LINE = 4
SPARE = 32
HALF = U // 2
SCALAR_CHUNKS = [(512, 256), (768, 128)]
LAST_START, LAST_WIDTH = 896, 128


def tile_picked_ydiffex_gate_p_kernel(
    tc, x_words, x_scales, w1, w2, old, unit, w3, offs, snd, oth, out
):
    nc = tc.nc
    with ExitStack() as ctx:
        keep = ctx.enter_context(tc.tile_pool(name="keep", bufs=1))
        psum = ctx.enter_context(tc.psum_pool(name="psum", bufs=1))

        def entries(list_tile, start, count):
            return list_tile[:, start // PER_COLUMN : (start + count) // PER_COLUMN]

        offs_sb = keep.tile([P, S // PER_COLUMN], U16, name="offs_sb")
        snd_sb = keep.tile([P, U // PER_COLUMN], U16, name="snd_sb")
        oth_sb = keep.tile([P, U // PER_COLUMN], U16, name="oth_sb")
        nc.sync.dma_start(offs_sb[:], offs)

        table_scales = keep.tile([P, T], U8, name="table_scales", align_bytes=64)
        nc.gpsimd.memset(table_scales[:].bitcast(I32), 0)
        for quad in range(4):
            nc.gpsimd.dma_start(
                table_scales[32 * quad : 32 * quad + 4 * PASSES, :].bitcast(I32),
                x_scales[:, 4 * quad : 4 * quad + 4, :].bitcast(I32),
            )

        def load_words(g):
            words = keep.tile([P, T], I32, name="table_words%d" % g, align_bytes=64)
            nc.sync.dma_start(words[:], x_words[g].rearrange("p n t -> p (n t)").bitcast(I32))
            return words

        def load_rows(w, g, label):
            raw = keep.tile([P, PACK, w.shape[1]], F32, name="raw_" + label, tag="raw_" + label, align_bytes=64)
            rows = w[g * P * PACK : (g + 1) * P * PACK, :]
            nc.sync.dma_start(raw[:], rows.rearrange("(p j) c -> p j c", j=PACK))
            return raw

        raw_w1, table_words = [], []
        for g in range(PASSES):
            raw_w1.append(load_rows(w1, g, "w1_%d" % g))
            table_words.append(load_words(g))
        nc.sync.dma_start(oth_sb[:], oth)
        nc.sync.dma_start(snd_sb[:], snd)
        raw_w2 = [load_rows(w2, g, "w2_%d" % g) for g in range(PASSES)]
        unit_sb = keep.tile([P, PACK], F32, name="unit_sb")
        nc.sync.dma_start(unit_sb[:], unit.rearrange("(p t) o -> p (t o)", t=PACK))
        old_rows = old.rearrange("(p t) r -> p t r", t=PACK)
        old_sb = []
        for pair in range(PACK // 2):
            kept = keep.tile([P, 2, U], F32, name="old%d" % pair)
            nc.sync.dma_start(kept[:], old_rows[:, 2 * pair : 2 * pair + 2, :])
            old_sb.append(kept)
        raw_w3 = load_rows(w3, 0, "w3")

        windows = {}
        for label in ("y", "z"):
            for t in range(PACK):
                window = keep.tile([P, S + SPARE], F32, name="window_%s%d" % (label, t))
                nc.vector.memset(window[:, S:], 0.0)
                windows[label, t] = window

        def deal_columns(raw, tag, *copies):
            grouped = keep.tile([P, H * PACK], BF16, name="grouped", tag=tag, align_bytes=64)
            dst = grouped[:].rearrange("p (t m j) -> p m j t", t=PACK, j=PACK)
            src = raw[:].rearrange("p j (m t) -> p m j t", t=PACK)
            share = P // len(copies)
            for index, copy in enumerate(copies):
                copy(dst[:, index * share : (index + 1) * share], src[:, index * share : (index + 1) * share])
            return grouped

        def scalar_copy(dst, src):
            nc.scalar.activation(dst, src, COPY)

        def quantize(grouped, label):
            width = grouped.shape[1] // PACK
            codes = keep.tile([P, width], U32, name="codes_" + label, tag="codes_" + label, align_bytes=64)
            scales = keep.tile([P, width], U8, name="scales_" + label, tag="scales_" + label, align_bytes=64)
            nc.vector.quantize_mx(out=codes[:].bitcast(FP8X4), scales=scales[:], in_=grouped[:])
            return codes, scales

        picked_words = []

        def pick_words(g, parts):
            picked = keep.tile([P, S], U32, name="picked_words%d" % g, align_bytes=64)
            width = S // parts
            for start in range(0, S, width):
                window = table_words[g][:].bitcast(U32)
                nc.vector.tensor_copy(picked[:, start : start + width], window.indirect(entries(offs_sb, start, width)))
            picked_words.append(picked)

        whole_planes = [(t, 0, S) for t in range(PACK)]

        def first_product_pass(accs, quantized, g, steps):
            codes, scales = quantized
            for t, lo, hi in steps:
                nc.tensor.matmul_mx(
                    out=accs[t][:, lo:hi],
                    lhsT=codes[:, t * P : (t + 1) * P].bitcast(FP8X4),
                    lhsT_scale=scales[:, t * P : (t + 1) * P],
                    rhs=picked_words[g][:, lo:hi].bitcast(FP8X4),
                    rhs_scale=picked_scales[4 * g : P, lo:hi],
                    start=(g == 0),
                    stop=(g == PASSES - 1 and hi == S),
                )

        acc_y = [psum.tile([P, S], F32, name="acc_y%d" % t, tag="bank%d" % t) for t in range(PACK)]
        acc_z = [psum.tile([P, S], F32, name="acc_z%d" % t, tag="bank%d" % (PACK + t)) for t in range(PACK)]

        pick_words(0, 1)
        quantized = quantize(deal_columns(raw_w1[0], "w1_0", scalar_copy), "w1_0")
        picked_scales = keep.tile([P, S], U8, name="picked_scales", tag="w1_0", align_bytes=64)
        nc.vector.tensor_copy(picked_scales[:], table_scales[:].indirect(offs_sb[:]))
        first_product_pass(acc_y, quantized, 0, whole_planes)
        quantized = quantize(deal_columns(raw_w1[1], "w1_1", nc.vector.tensor_copy, scalar_copy), "w1_1")
        pick_words(1, 2)
        halves = [(t, lo, lo + S // 2) for lo in (0, S // 2) for t in range(2)]
        first_product_pass(acc_y, quantized, 1, halves + whole_planes[2:])

        def negated_other(t, h, fetched):
            window = windows["y", t][:]
            nc.scalar.activation(fetched, window.indirect(entries(oth_sb, h * HALF, HALF)), COPY, scale=-1.0)
            return fetched

        def stage(tag, width=HALF):
            return keep.tile([P, width], F32, name="stage", tag=tag, align_bytes=64)[:]

        def difference(dst, t, h, negated):
            window = windows["y", t][:]
            nc.vector.tensor_tensor(dst, window.indirect(entries(snd_sb, h * HALF, HALF)), negated, ADD)

        diff_first = {}

        def first_difference(t, negated, tag):
            diff_first[t] = stage(tag)
            difference(diff_first[t], t, 0, negated)

        scalar_copy(windows["y", 0][:, :S], acc_y[0][:])
        for t in (1, 2, 3):
            nc.vector.tensor_copy(windows["y", t][:, :S], acc_y[t][:])
        first_difference(0, negated_other(0, 0, stage("other00")), "diff00")
        grouped = deal_columns(raw_w2[0], "other00", nc.vector.tensor_copy)
        first_difference(1, negated_other(1, 0, stage("other10")), "raw_w2_0")
        first_product_pass(acc_z, quantize(grouped, "w2_0"), 0, whole_planes)
        diff_second = keep.tile([P, PACK, HALF], F32, name="diff_second", tag="other00", align_bytes=64)
        difference(diff_second[:, 0, :], 0, 1, negated_other(0, 1, stage("other01")))
        difference(diff_second[:, 1, :], 1, 1, negated_other(1, 1, stage("other11")))
        grouped = deal_columns(raw_w2[1], "other10", scalar_copy)
        late = stage("raw_w2_1", 3 * HALF)
        negated = negated_other(2, 0, late[:, :HALF])
        first_product_pass(acc_z, quantize(grouped, "w2_1"), 1, whole_planes)
        first_difference(2, negated, "other10")
        difference(diff_second[:, 2, :], 2, 1, negated_other(2, 1, late[:, HALF : 2 * HALF]))
        difference(diff_second[:, 3, :], 3, 1, negated_other(3, 1, late[:, 2 * HALF :]))
        for t in range(PACK):
            nc.scalar.activation(windows["z", t][:, :S], acc_z[t][:], COPY, scale=unit_sb[:, t : t + 1])
        negated = negated_other(3, 0, stage("codes_w2_1"))

        def weigh_fused(dst, t, r0, n, diff):
            nc.vector.tensor_tensor(dst, windows["z", t][:].indirect(entries(oth_sb, r0, n)), diff, MULT)

        wex_first = keep.tile([P, PACK, HALF], F32, name="wex_first")
        for t in range(PACK - 1):
            weigh_fused(wex_first[:, t, :], t, 0, HALF, diff_first[t])
        first_difference(3, negated, "diff30")
        weigh_fused(wex_first[:, 3, :], 3, 0, HALF, diff_first[3])

        scaled_old = keep.tile([P, PACK, U], F32, name="scaled_old", tag="scales_w2_1", align_bytes=64)
        for t in range(PACK):
            nc.scalar.activation(scaled_old[:, t, :], old_sb[t // 2][:, t % 2, :], COPY, scale=unit_sb[:, t : t + 1])

        grouped_w3 = keep.tile([P, N * PACK], BF16, name="grouped_w3", tag="codes_w2_1", align_bytes=64)
        scalar_copy(
            grouped_w3[:].rearrange("p (c i j) -> p c j i", i=LINE, j=PACK),
            raw_w3[:].rearrange("p j (c i) -> p c j i", i=LINE),
        )
        w3_codes, w3_scales = quantize(grouped_w3, "w3")

        def fetch_gates(r0, n):
            gates = keep.tile([P, PACK, n], F32, name="gates%d" % r0)
            for t in range(PACK):
                scalar_copy(gates[:, t, :], windows["z", t][:].indirect(entries(oth_sb, r0, n)))
            return gates

        def weigh_fetched(r0, n, gates):
            wex = keep.tile([P, PACK, n], F32, name="wex%d" % r0)
            nc.vector.tensor_tensor(wex[:], gates[:], diff_second[:, :, r0 - HALF : r0 - HALF + n], MULT)
            return wex

        def last_product(r0, n, wex, bank, copy_out):
            grouped_hid = keep.tile([P, n * PACK], BF16, name="grouped_hid%d" % r0, align_bytes=64)
            nc.vector.tensor_tensor(
                grouped_hid[:].rearrange("p (c i t) -> p c t i", i=LINE, t=PACK),
                wex[:].rearrange("p t (c i) -> p c t i", i=LINE),
                scaled_old[:, :, r0 : r0 + n].rearrange("p t (c i) -> p c t i", i=LINE),
                ADD,
            )
            codes, scales = quantize(grouped_hid, "hid%d" % r0)
            acc = psum.tile([P, n], F32, name="acc_out", tag="bank%d" % bank)
            nc.tensor.matmul_mx(
                out=acc[:],
                lhsT=w3_codes[:].bitcast(FP8X4),
                lhsT_scale=w3_scales[:],
                rhs=codes[:].bitcast(FP8X4),
                rhs_scale=scales[:],
                start=True,
                stop=True,
            )
            result = keep.tile([P, n], F32, name="result%d" % r0)
            copy_out(result[:], acc[:])
            nc.sync.dma_start(out[:, r0 : r0 + n], result[:])

        wex_last = keep.tile([P, PACK, LAST_WIDTH], F32, name="wex_last")
        for t in range(PACK):
            weigh_fused(wex_last[:, t, :], t, LAST_START, LAST_WIDTH, diff_second[:, t, LAST_START - HALF :])
        fetched_gates = [fetch_gates(r0, n) for r0, n in SCALAR_CHUNKS]

        last_product(0, HALF, wex_first, 0, nc.scalar.copy)
        for index, (r0, n) in enumerate(SCALAR_CHUNKS):
            last_product(r0, n, weigh_fetched(r0, n, fetched_gates[index]), index + 1, nc.scalar.copy)
        last_product(LAST_START, LAST_WIDTH, wex_last, PACK - 1, nc.vector.tensor_copy)
